import numpy as np
import ml_dtypes


def mxq(x, axis, fmt="e4m3"):
    dtype, down = {"e4m3": (ml_dtypes.float8_e4m3fn, 7), "e5m2": (ml_dtypes.float8_e5m2, 14)}[fmt]
    v = np.moveaxis(np.asarray(x, np.float32).astype(ml_dtypes.bfloat16).astype(np.float64), axis, -1)
    blocks = v.reshape(v.shape[:-1] + (-1, 32))
    amax = np.abs(blocks).max(-1, keepdims=True)
    byte = np.maximum(np.where(amax > 0, np.frexp(amax)[1] - 1 + 127, 0) - down, 1)
    scale = np.exp2(byte - 127.0)
    codes = (blocks / scale).astype(np.float32).astype(dtype).astype(np.float64)
    return np.moveaxis((codes * scale).reshape(v.shape), -1, axis)


WIDE = False


def mx_kscale(k):
    if not WIDE:
        return np.ones(k)
    levels = np.array([10, -10, 5, -5, 0])
    if k % 512:
        return np.exp2(np.random.permutation(np.resize(levels, k // 32))).repeat(32)
    a = np.empty((k // 512, 16))
    for p in range(k // 512):
        a[p, :8] = np.random.permutation(np.resize(levels, 8))
        for g in range(8):
            far = levels[np.abs(levels - a[p, g]) >= 10]
            a[p, g + 8] = far[np.random.randint(len(far))]
    return np.exp2(a.ravel()).repeat(32)


def f64(x):
    return np.asarray(x).astype(np.float64)


def striped(idx):
    return np.tile(idx.reshape(-1, 16).T, (8, 1)).astype(np.uint16)


def unstriped(offs):
    return offs[:16].T.reshape(-1).astype(np.int64)


def pack_weight(w):
    k, n = w.shape
    w = f64(np.asarray(w, np.float32).astype(ml_dtypes.bfloat16)).reshape(k // 32, 32, n)
    amax = np.abs(w).max(1)
    byte = np.clip(np.where(amax > 0, np.frexp(amax)[1] - 1 + 127 - 7, 1), 1, 254)
    scaled = (w * np.exp2(127.0 - byte)[:, None, :]).reshape(k, n).astype(np.float32)
    words = np.ascontiguousarray(scaled.reshape(k // 512, 128, 4, n).transpose(0, 1, 3, 2)).astype(ml_dtypes.float8_e4m3fn).view(np.uint8)
    return words, np.ascontiguousarray(byte.astype(np.uint8).reshape(k // 512, 16, n))


def unpack_weight(words, scales):
    g, p, n, _ = words.shape
    vals = np.ascontiguousarray(words).view(ml_dtypes.float8_e4m3fn).astype(np.float64) * np.repeat(np.exp2(scales.astype(np.float64) - 127.0), 8, axis=1)[..., None]
    return vals.transpose(0, 1, 3, 2).reshape(g * 512, n)


K, T, S, H, N = 512, 1024, 512, 512, 256


def setup_inputs():
    n = np.random.standard_normal
    s = mx_kscale(K)[:, None]
    u = mx_kscale(H)
    packed_xT = pack_weight(n((K, T)) * s)
    return {
        "x_words": packed_xT[0],
        "x_scales": packed_xT[1],
        "w1": (n((K, H)) / np.sqrt(K) / s * u).astype(np.float32),
        "w2": (n((H, N)) / np.sqrt(H) / u[:, None]).astype(np.float32),
        "offs": striped(np.random.permutation(T)[:S]),
    }


def reference(x_words, x_scales, w1, w2, offs):
    xq = unpack_weight(x_words, x_scales)[:, unstriped(offs)]
    h = mxq(f64(w1), 0, "e4m3").T @ xq
    z = h - h.mean(axis=1, keepdims=True)
    return mxq(f64(w2), 0, "e4m3").T @ mxq(z, 0, "e4m3")

@@ -1,0 +1,177 @@
+from contextlib import ExitStack
+
+import concourse.mybir as mybir
+
+K, T, S, H, N = 512, 1024, 512, 512, 256
+FLOPS = 2 * K * H * S + 2 * H * N * S
+
+F32 = mybir.dt.float32
+BF16 = mybir.dt.bfloat16
+I32 = mybir.dt.int32
+U32 = mybir.dt.uint32
+U16 = mybir.dt.uint16
+U8 = mybir.dt.uint8
+FP8X4 = mybir.dt.float8_e4m3fn_x4
+ACT = mybir.ActivationFunctionType
+ALU = mybir.AluOpType
+AXIS = mybir.AxisListType
+
+P = 128
+PACK = 4
+CH = 128
+NCH = S // CH
+LIST_COLS = CH // 16
+SPLIT = 44
+
+
+def tile_picked_deepset_none_p_kernel(tc, x_words, x_scales, w1, w2, offs, out):
+    nc = tc.nc
+    with ExitStack() as ctx:
+        keep = ctx.enter_context(tc.tile_pool(name="keep", bufs=1))
+        psum = ctx.enter_context(tc.psum_pool(name="psum", bufs=1))
+
+        offsets = keep.tile([P, S // 16], U16, name="offsets")
+        xs_table = keep.tile([P, T], U8, name="xs_table", align_bytes=64)
+        xw_table = keep.tile([P, T], I32, name="xw_table", align_bytes=64)
+        w1_raw = [keep.tile([P, 2, H], F32, name="w1_raw%d" % u, align_bytes=64) for u in range(2)]
+        w2_raw = keep.tile([P, PACK, N], F32, name="w2_raw", align_bytes=64)
+
+        nc.vector.memset(xs_table[:].bitcast(I32), 0)
+        w1_rows = w1.rearrange("(p j) c -> p j c", j=PACK)
+        nc.sync.dma_start(w1_raw[0][:], w1_rows[:, 0:2, :])
+        nc.sync.dma_start(offsets[:], offs)
+        for q in range(4):
+            nc.sync.dma_start(
+                xs_table[32 * q : 32 * q + 4, :].bitcast(I32), x_scales[0, 4 * q : 4 * q + 4, :].bitcast(I32)
+            )
+        nc.sync.dma_start(xw_table[:], x_words[0].rearrange("p n t -> p (n t)").bitcast(I32))
+        nc.sync.dma_start(w1_raw[1][:], w1_rows[:, 2:4, :])
+        nc.sync.dma_start(w2_raw[:], w2.rearrange("(p j) n -> p j n", j=PACK))
+
+        xs = keep.tile([P, S], U8, name="xs", align_bytes=64)
+        nc.vector.tensor_copy(xs[:], xs_table[:].indirect(offsets[:]))
+
+        xw = []
+        for c in range(NCH):
+            words = keep.tile([P, CH], U32, name="xw%d" % c, align_bytes=64)
+            nc.vector.tensor_copy(
+                words[:], xw_table[:].bitcast(U32).indirect(offsets[:, c * LIST_COLS : (c + 1) * LIST_COLS])
+            )
+            xw.append(words)
+
+        w1_bf = keep.tile([P, PACK * P * PACK], BF16, name="w1_bf", align_bytes=64)
+        w1_dst = w1_bf[:].rearrange("p (t a b j) -> p a t b j", t=PACK, b=2, j=PACK)
+        w1_src = [w1_raw[u][:].rearrange("p j (a b t) -> p a t b j", b=2, t=PACK) for u in range(2)]
+        nc.scalar.copy(w1_dst[:, :, :, :, 0:2], w1_src[0])
+        nc.vector.tensor_copy(w1_dst[:, :SPLIT, :, :, 2:4], w1_src[1][:, :SPLIT])
+        nc.scalar.copy(w1_dst[:, SPLIT:, :, :, 2:4], w1_src[1][:, SPLIT:])
+        w1_codes, w1_scales = [], []
+        for t in range(PACK):
+            codes = keep.tile([P, P], U32, name="w1_codes%d" % t, align_bytes=64)
+            scales = keep.tile([P, P], U8, name="w1_scales%d" % t, align_bytes=64)
+            nc.vector.quantize_mx(
+                out=codes[:].bitcast(FP8X4), scales=scales[:], in_=w1_bf[:, t * P * PACK : (t + 1) * P * PACK]
+            )
+            w1_codes.append(codes)
+            w1_scales.append(scales)
+
+        sums = keep.tile([P, NCH, PACK], F32, name="sums")
+        junk = keep.tile([P, CH], BF16, name="junk")
+        h = []
+        for c in range(NCH):
+            bank = psum.tile([P, PACK, CH], F32, name="h%d" % c)
+            for t in range(PACK):
+                nc.tensor.matmul_mx(
+                    out=bank[:, t, :],
+                    lhsT=w1_codes[t][:].bitcast(FP8X4),
+                    lhsT_scale=w1_scales[t][:],
+                    rhs=xw[c][:].bitcast(FP8X4),
+                    rhs_scale=xs[:, c * CH : (c + 1) * CH],
+                    start=True,
+                    stop=True,
+                )
+            h.append(bank)
+
+        w2_bf = keep.tile([P, N * PACK], BF16, name="w2_bf", align_bytes=64)
+        nc.vector.tensor_copy(
+            w2_bf[:].rearrange("p (a i j) -> p a j i", i=4, j=PACK),
+            w2_raw[:].rearrange("p j (a i) -> p a j i", i=4),
+        )
+        w2_codes = keep.tile([P, N], U32, name="w2_codes", align_bytes=64)
+        w2_scales = keep.tile([P, N], U8, name="w2_scales", align_bytes=64)
+        nc.vector.quantize_mx(out=w2_codes[:].bitcast(FP8X4), scales=w2_scales[:], in_=w2_bf[:])
+
+        for c in range(NCH):
+            if c % 2 == 0:
+                for t in range(PACK):
+                    nc.scalar.activation(junk[:], h[c][:, t, :], ACT.Copy, accum_out=sums[:, c, t : t + 1])
+            else:
+                nc.vector.tensor_reduce(sums[:, c, :], h[c][:], AXIS.X, ALU.add)
+
+        total = keep.tile([P, PACK], F32, name="total")
+        nc.vector.tensor_reduce(total[:], sums[:].rearrange("p c t -> p t c"), AXIS.X, ALU.add)
+
+        neg_mean = keep.tile([P, PACK], F32, name="neg_mean")
+        nc.scalar.activation(neg_mean[:], total[:], ACT.Copy, scale=-1.0 / S)
+
+        z_bf = [keep.tile([P, CH * PACK], BF16, name="z_bf%d" % c, align_bytes=64) for c in range(NCH)]
+        out_rows = out.rearrange("(a p) s -> p a s", p=P)
+
+        def centre_on_vector(c):
+            nc.vector.scalar_tensor_tensor(
+                out=z_bf[c][:].rearrange("p (n t) -> p n t", t=PACK),
+                in0=total[:].unsqueeze(1).to_broadcast([P, CH, PACK]),
+                scalar=-1.0 / S,
+                in1=h[c][:].rearrange("p t n -> p n t"),
+                op0=ALU.mult,
+                op1=ALU.add,
+            )
+
+        def centre_on_scalar(c):
+            planes = keep.tile([P, PACK, CH], BF16, name="planes%d" % c, align_bytes=64)
+            for t in range(PACK):
+                nc.scalar.activation(planes[:, t, :], h[c][:, t, :], ACT.Identity, bias=neg_mean[:, t : t + 1])
+            nc.scalar.copy(
+                z_bf[c][:].rearrange("p (a i t) -> p a t i", i=4, t=PACK),
+                planes[:].rearrange("p t (a i) -> p a t i", i=4),
+            )
+
+        banks = {}
+
+        def second_product(c):
+            z_codes = keep.tile([P, CH], U32, name="z_codes%d" % c, align_bytes=64)
+            z_scales = keep.tile([P, CH], U8, name="z_scales%d" % c, align_bytes=64)
+            nc.vector.quantize_mx(out=z_codes[:].bitcast(FP8X4), scales=z_scales[:], in_=z_bf[c][:])
+            bank = psum.tile([P, N // P, CH], F32, name="o%d" % c)
+            for a in range(N // P):
+                nc.tensor.matmul_mx(
+                    out=bank[:, a, :],
+                    lhsT=w2_codes[:, a * P : (a + 1) * P].bitcast(FP8X4),
+                    lhsT_scale=w2_scales[:, a * P : (a + 1) * P],
+                    rhs=z_codes[:].bitcast(FP8X4),
+                    rhs_scale=z_scales[:],
+                    start=True,
+                    stop=True,
+                )
+            banks[c] = bank
+
+        def store(c, on_vector):
+            result = keep.tile([P, N // P, CH], F32, name="result%d" % c)
+            if on_vector:
+                nc.vector.tensor_copy(result[:], banks[c][:])
+            else:
+                nc.scalar.copy(result[:], banks[c][:])
+            nc.sync.dma_start(out_rows[:, :, c * CH : (c + 1) * CH], result[:])
+
+        centre_on_scalar(2)
+        centre_on_vector(0)
+        centre_on_vector(1)
+        second_product(0)
+        centre_on_vector(3)
+        second_product(1)
+        second_product(2)
+        second_product(3)
+        store(0, False)
+        store(1, False)
+        store(2, False)
+        store(3, True)

@@ -21,7 +21,6 @@ PACK = 4
 CH = 128
 NCH = S // CH
 LIST_COLS = CH // 16
-SPLIT = 44
 
 
 def tile_picked_deepset_none_p_kernel(tc, x_words, x_scales, w1, w2, offs, out):
@@ -33,23 +32,47 @@ def tile_picked_deepset_none_p_kernel(tc, x_words, x_scales, w1, w2, offs, out):
         offsets = keep.tile([P, S // 16], U16, name="offsets")
         xs_table = keep.tile([P, T], U8, name="xs_table", align_bytes=64)
         xw_table = keep.tile([P, T], I32, name="xw_table", align_bytes=64)
-        w1_raw = [keep.tile([P, 2, H], F32, name="w1_raw%d" % u, align_bytes=64) for u in range(2)]
+        w1_raw = [keep.tile([P, PACK, H // 2], F32, name="w1_raw%d" % u, align_bytes=64) for u in range(2)]
         w2_raw = keep.tile([P, PACK, N], F32, name="w2_raw", align_bytes=64)
 
         nc.vector.memset(xs_table[:].bitcast(I32), 0)
         w1_rows = w1.rearrange("(p j) c -> p j c", j=PACK)
-        nc.sync.dma_start(w1_raw[0][:], w1_rows[:, 0:2, :])
+        nc.sync.dma_start(w1_raw[0][:], w1_rows[:, :, : H // 2])
         nc.sync.dma_start(offsets[:], offs)
         for q in range(4):
             nc.sync.dma_start(
                 xs_table[32 * q : 32 * q + 4, :].bitcast(I32), x_scales[0, 4 * q : 4 * q + 4, :].bitcast(I32)
             )
+        nc.sync.dma_start(w1_raw[1][:], w1_rows[:, :, H // 2 :])
         nc.sync.dma_start(xw_table[:], x_words[0].rearrange("p n t -> p (n t)").bitcast(I32))
-        nc.sync.dma_start(w1_raw[1][:], w1_rows[:, 2:4, :])
-        nc.sync.dma_start(w2_raw[:], w2.rearrange("(p j) n -> p j n", j=PACK))
+        w2_rows = w2.rearrange("(g t r) n -> t g r n", t=PACK, r=4)
+        for t in range(PACK):
+            nc.sync.dma_start(w2_raw[:, t, :], w2_rows[t])
 
         xs = keep.tile([P, S], U8, name="xs", align_bytes=64)
         nc.vector.tensor_copy(xs[:], xs_table[:].indirect(offsets[:]))
+
+        w1_bf = {}
+
+        def deal_w1(copy, u, t0, t1):
+            dealt = keep.tile([P, (t1 - t0) * 256], BF16, name="w1_bf%d_%d" % (u, t0), align_bytes=64)
+            copy(
+                dealt[:].rearrange("p (t g r j) -> p g t j r", g=16, r=4, j=PACK),
+                w1_raw[u][:].rearrange("p j (g t r) -> p g t j r", t=PACK, r=4)[:, :, t0:t1],
+            )
+            for t in range(t0, t1):
+                w1_bf[u, t] = dealt[:, (t - t0) * 256 : (t - t0 + 1) * 256]
+
+        deal_w1(nc.scalar.copy, 0, 0, 4)
+        deal_w1(nc.vector.tensor_copy, 1, 0, 2)
+        deal_w1(nc.scalar.copy, 1, 2, 4)
+        w1_codes = [keep.tile([P, P], U32, name="w1_codes%d" % t, align_bytes=64) for t in range(PACK)]
+        w1_scales = [keep.tile([P, P], U8, name="w1_scales%d" % t, align_bytes=64) for t in range(PACK)]
+        for u, t in ((0, 0), (0, 1), (0, 2), (0, 3), (1, 0), (1, 1), (1, 2), (1, 3)):
+            cols = slice(64 * u, 64 * (u + 1))
+            nc.vector.quantize_mx(
+                out=w1_codes[t][:, cols].bitcast(FP8X4), scales=w1_scales[t][:, cols], in_=w1_bf[u, t]
+            )
 
         xw = []
         for c in range(NCH):
@@ -59,57 +82,53 @@ def tile_picked_deepset_none_p_kernel(tc, x_words, x_scales, w1, w2, offs, out):
             )
             xw.append(words)
 
-        w1_bf = keep.tile([P, PACK * P * PACK], BF16, name="w1_bf", align_bytes=64)
-        w1_dst = w1_bf[:].rearrange("p (t a b j) -> p a t b j", t=PACK, b=2, j=PACK)
-        w1_src = [w1_raw[u][:].rearrange("p j (a b t) -> p a t b j", b=2, t=PACK) for u in range(2)]
-        nc.scalar.copy(w1_dst[:, :, :, :, 0:2], w1_src[0])
-        nc.vector.tensor_copy(w1_dst[:, :SPLIT, :, :, 2:4], w1_src[1][:, :SPLIT])
-        nc.scalar.copy(w1_dst[:, SPLIT:, :, :, 2:4], w1_src[1][:, SPLIT:])
-        w1_codes, w1_scales = [], []
-        for t in range(PACK):
-            codes = keep.tile([P, P], U32, name="w1_codes%d" % t, align_bytes=64)
-            scales = keep.tile([P, P], U8, name="w1_scales%d" % t, align_bytes=64)
-            nc.vector.quantize_mx(
-                out=codes[:].bitcast(FP8X4), scales=scales[:], in_=w1_bf[:, t * P * PACK : (t + 1) * P * PACK]
+        def first_product(dst, t, c):
+            nc.tensor.matmul_mx(
+                out=dst,
+                lhsT=w1_codes[t][:].bitcast(FP8X4),
+                lhsT_scale=w1_scales[t][:],
+                rhs=xw[c][:].bitcast(FP8X4),
+                rhs_scale=xs[:, c * CH : (c + 1) * CH],
+                start=True,
+                stop=True,
             )
-            w1_codes.append(codes)
-            w1_scales.append(scales)
 
-        sums = keep.tile([P, NCH, PACK], F32, name="sums")
-        junk = keep.tile([P, CH], BF16, name="junk")
+        last = NCH - 1
         h = []
-        for c in range(NCH):
-            bank = psum.tile([P, PACK, CH], F32, name="h%d" % c)
+        for c in range(last):
+            bank = psum.tile([P, PACK, CH], F32, name="h%d" % c, tag="bank%d" % c)
             for t in range(PACK):
-                nc.tensor.matmul_mx(
-                    out=bank[:, t, :],
-                    lhsT=w1_codes[t][:].bitcast(FP8X4),
-                    lhsT_scale=w1_scales[t][:],
-                    rhs=xw[c][:].bitcast(FP8X4),
-                    rhs_scale=xs[:, c * CH : (c + 1) * CH],
-                    start=True,
-                    stop=True,
-                )
+                first_product(bank[:, t, :], t, c)
             h.append(bank)
+        h_last = []
+        for u in range(2):
+            bank = psum.tile([P, 2, CH], F32, name="h_last%d" % u, tag="bank%d" % (last + u))
+            for e in range(2):
+                first_product(bank[:, e, :], 2 * u + e, last)
+            h_last.append(bank)
 
         w2_bf = keep.tile([P, N * PACK], BF16, name="w2_bf", align_bytes=64)
-        nc.vector.tensor_copy(
+        nc.scalar.copy(
             w2_bf[:].rearrange("p (a i j) -> p a j i", i=4, j=PACK),
             w2_raw[:].rearrange("p j (a i) -> p a j i", i=4),
         )
+
+        sums = keep.tile([P, NCH * PACK], F32, name="sums")
+        junk = keep.tile([P, PACK * CH], BF16, name="junk")
+        for c in (0, 1):
+            nc.vector.tensor_reduce(sums[:, PACK * c : PACK * (c + 1)], h[c][:], AXIS.X, ALU.add)
         w2_codes = keep.tile([P, N], U32, name="w2_codes", align_bytes=64)
         w2_scales = keep.tile([P, N], U8, name="w2_scales", align_bytes=64)
         nc.vector.quantize_mx(out=w2_codes[:].bitcast(FP8X4), scales=w2_scales[:], in_=w2_bf[:])
-
-        for c in range(NCH):
-            if c % 2 == 0:
-                for t in range(PACK):
-                    nc.scalar.activation(junk[:], h[c][:, t, :], ACT.Copy, accum_out=sums[:, c, t : t + 1])
-            else:
-                nc.vector.tensor_reduce(sums[:, c, :], h[c][:], AXIS.X, ALU.add)
+        for t in range(PACK):
+            nc.scalar.activation(
+                junk[:, t * CH : (t + 1) * CH], h[2][:, t, :], ACT.Copy, accum_out=sums[:, 8 + t : 9 + t]
+            )
+        for u in range(2):
+            nc.vector.tensor_reduce(sums[:, 12 + 2 * u : 14 + 2 * u], h_last[u][:], AXIS.X, ALU.add)
 
         total = keep.tile([P, PACK], F32, name="total")
-        nc.vector.tensor_reduce(total[:], sums[:].rearrange("p c t -> p t c"), AXIS.X, ALU.add)
+        nc.vector.tensor_reduce(total[:], sums[:].rearrange("p (c t) -> p t c", t=PACK), AXIS.X, ALU.add)
 
         neg_mean = keep.tile([P, PACK], F32, name="neg_mean")
         nc.scalar.activation(neg_mean[:], total[:], ACT.Copy, scale=-1.0 / S)
@@ -127,25 +146,23 @@ def tile_picked_deepset_none_p_kernel(tc, x_words, x_scales, w1, w2, offs, out):
                 op1=ALU.add,
             )
 
-        def centre_on_scalar(c):
-            planes = keep.tile([P, PACK, CH], BF16, name="planes%d" % c, align_bytes=64)
-            for t in range(PACK):
-                nc.scalar.activation(planes[:, t, :], h[c][:, t, :], ACT.Identity, bias=neg_mean[:, t : t + 1])
-            nc.scalar.copy(
-                z_bf[c][:].rearrange("p (a i t) -> p a t i", i=4, t=PACK),
-                planes[:].rearrange("p t (a i) -> p a t i", i=4),
+        planes = keep.tile([P, PACK * CH], BF16, name="planes", align_bytes=64)
+        for t in range(PACK):
+            nc.scalar.activation(
+                planes[:, t * CH : (t + 1) * CH], h_last[t // 2][:, t % 2, :], ACT.Identity, bias=neg_mean[:, t : t + 1]
             )
+        nc.scalar.copy(
+            z_bf[last][:].rearrange("p (a i t) -> p a t i", i=4, t=PACK),
+            planes[:].rearrange("p (t a i) -> p a t i", t=PACK, i=4),
+        )
 
-        banks = {}
-
-        def second_product(c):
+        def second_product(c, dsts):
             z_codes = keep.tile([P, CH], U32, name="z_codes%d" % c, align_bytes=64)
             z_scales = keep.tile([P, CH], U8, name="z_scales%d" % c, align_bytes=64)
             nc.vector.quantize_mx(out=z_codes[:].bitcast(FP8X4), scales=z_scales[:], in_=z_bf[c][:])
-            bank = psum.tile([P, N // P, CH], F32, name="o%d" % c)
             for a in range(N // P):
                 nc.tensor.matmul_mx(
-                    out=bank[:, a, :],
+                    out=dsts[a],
                     lhsT=w2_codes[:, a * P : (a + 1) * P].bitcast(FP8X4),
                     lhsT_scale=w2_scales[:, a * P : (a + 1) * P],
                     rhs=z_codes[:].bitcast(FP8X4),
@@ -153,25 +170,27 @@ def tile_picked_deepset_none_p_kernel(tc, x_words, x_scales, w1, w2, offs, out):
                     start=True,
                     stop=True,
                 )
-            banks[c] = bank
 
-        def store(c, on_vector):
+        def finish(c):
+            bank = psum.tile([P, N // P, CH], F32, name="o%d" % c, tag="obank%d" % c)
+            second_product(c, [bank[:, 0, :], bank[:, 1, :]])
             result = keep.tile([P, N // P, CH], F32, name="result%d" % c)
-            if on_vector:
-                nc.vector.tensor_copy(result[:], banks[c][:])
-            else:
-                nc.scalar.copy(result[:], banks[c][:])
+            nc.scalar.copy(result[:], bank[:])
             nc.sync.dma_start(out_rows[:, :, c * CH : (c + 1) * CH], result[:])
 
-        centre_on_scalar(2)
+        def finish_split(c):
+            halves = [psum.tile([P, CH], F32, name="o%d_%d" % (c, a), tag="bank%d" % a) for a in range(2)]
+            second_product(c, [halves[0][:], halves[1][:]])
+            results = [keep.tile([P, CH], F32, name="result%d_%d" % (c, a)) for a in range(2)]
+            nc.vector.tensor_copy(results[0][:], halves[0][:])
+            nc.sync.dma_start(out_rows[:, 0, c * CH : (c + 1) * CH], results[0][:])
+            nc.scalar.copy(results[1][:], halves[1][:])
+            nc.scalar.dma_start(out_rows[:, 1, c * CH : (c + 1) * CH], results[1][:])
+
         centre_on_vector(0)
         centre_on_vector(1)
-        second_product(0)
-        centre_on_vector(3)
-        second_product(1)
-        second_product(2)
-        second_product(3)
-        store(0, False)
-        store(1, False)
-        store(2, False)
-        store(3, True)
+        finish(0)
+        finish(1)
+        centre_on_vector(2)
+        finish(3)
+        finish_split(2)

@@ -27,13 +27,14 @@ def tile_picked_deepset_none_p_kernel(tc, x_words, x_scales, w1, w2, offs, out):
     nc = tc.nc
     with ExitStack() as ctx:
         keep = ctx.enter_context(tc.tile_pool(name="keep", bufs=1))
+        reuse = ctx.enter_context(tc.tile_pool(name="reuse", bufs=1))
         psum = ctx.enter_context(tc.psum_pool(name="psum", bufs=1))
 
         offsets = keep.tile([P, S // 16], U16, name="offsets")
-        xs_table = keep.tile([P, T], U8, name="xs_table", align_bytes=64)
+        xs_table = reuse.tile([P, T], U8, name="xs_table", offset=0, align_bytes=64)
         xw_table = keep.tile([P, T], I32, name="xw_table", align_bytes=64)
         w1_raw = [keep.tile([P, PACK, H // 2], F32, name="w1_raw%d" % u, align_bytes=64) for u in range(2)]
-        w2_raw = keep.tile([P, PACK, N], F32, name="w2_raw", align_bytes=64)
+        w2_raw = keep.tile([P, PACK, N], F32, name="w2_raw", tag="w2_raw", align_bytes=64)
 
         nc.vector.memset(xs_table[:].bitcast(I32), 0)
         w1_rows = w1.rearrange("(p j) c -> p j c", j=PACK)
@@ -54,8 +55,7 @@ def tile_picked_deepset_none_p_kernel(tc, x_words, x_scales, w1, w2, offs, out):
 
         w1_bf = {}
 
-        def deal_w1(copy, u, t0, t1):
-            dealt = keep.tile([P, (t1 - t0) * 256], BF16, name="w1_bf%d_%d" % (u, t0), align_bytes=64)
+        def deal_w1(copy, u, t0, t1, dealt):
             copy(
                 dealt[:].rearrange("p (t g r j) -> p g t j r", g=16, r=4, j=PACK),
                 w1_raw[u][:].rearrange("p j (g t r) -> p g t j r", t=PACK, r=4)[:, :, t0:t1],
@@ -63,31 +63,35 @@ def tile_picked_deepset_none_p_kernel(tc, x_words, x_scales, w1, w2, offs, out):
             for t in range(t0, t1):
                 w1_bf[u, t] = dealt[:, (t - t0) * 256 : (t - t0 + 1) * 256]
 
-        deal_w1(nc.scalar.copy, 0, 0, 4)
-        deal_w1(nc.vector.tensor_copy, 1, 0, 2)
-        deal_w1(nc.scalar.copy, 1, 2, 4)
+        w1_first = keep.tile([P, 1024], BF16, name="w1_first", align_bytes=64)
+        w1_middle = reuse.tile([P, 512], BF16, name="w1_middle", offset=512, align_bytes=64)
+        w1_last = keep.tile([P, 512], BF16, name="w1_last", tag="w1_last", align_bytes=64)
+        deal_w1(nc.scalar.copy, 0, 0, 4, w1_first)
+        deal_w1(nc.vector.tensor_copy, 1, 0, 2, w1_middle)
+        deal_w1(nc.scalar.copy, 1, 2, 4, w1_last)
         w1_codes = [keep.tile([P, P], U32, name="w1_codes%d" % t, align_bytes=64) for t in range(PACK)]
-        w1_scales = [keep.tile([P, P], U8, name="w1_scales%d" % t, align_bytes=64) for t in range(PACK)]
+        w1_scales = reuse.tile([P, H], U8, name="w1_scales", offset=0, align_bytes=64)
         for u, t in ((0, 0), (0, 1), (0, 2), (0, 3), (1, 0), (1, 1), (1, 2), (1, 3)):
             cols = slice(64 * u, 64 * (u + 1))
             nc.vector.quantize_mx(
-                out=w1_codes[t][:, cols].bitcast(FP8X4), scales=w1_scales[t][:, cols], in_=w1_bf[u, t]
+                out=w1_codes[t][:, cols].bitcast(FP8X4), scales=w1_scales[:, t * P + 64 * u : t * P + 64 * (u + 1)], in_=w1_bf[u, t]
             )
 
-        xw = []
+        xw_first = reuse.tile([P, CH], U32, name="xw_first", offset=512, align_bytes=64)
+        xw_rest = keep.tile([P, S - CH], U32, name="xw_rest", tag="w1_last", align_bytes=64)
+        xw = [xw_first[:]] + [xw_rest[:, c * CH : (c + 1) * CH] for c in range(NCH - 1)]
         for c in range(NCH):
-            words = keep.tile([P, CH], U32, name="xw%d" % c, align_bytes=64)
             nc.vector.tensor_copy(
-                words[:], xw_table[:].bitcast(U32).indirect(offsets[:, c * LIST_COLS : (c + 1) * LIST_COLS])
+                xw[c],
+                xw_table[:].bitcast(U32).indirect(offsets[:, c * LIST_COLS : (c + 1) * LIST_COLS]),
             )
-            xw.append(words)
 
         def first_product(dst, t, c):
             nc.tensor.matmul_mx(
                 out=dst,
                 lhsT=w1_codes[t][:].bitcast(FP8X4),
-                lhsT_scale=w1_scales[t][:],
-                rhs=xw[c][:].bitcast(FP8X4),
+                lhsT_scale=w1_scales[:, t * P : (t + 1) * P],
+                rhs=xw[c].bitcast(FP8X4),
                 rhs_scale=xs[:, c * CH : (c + 1) * CH],
                 start=True,
                 stop=True,
@@ -114,7 +118,7 @@ def tile_picked_deepset_none_p_kernel(tc, x_words, x_scales, w1, w2, offs, out):
         )
 
         sums = keep.tile([P, NCH * PACK], F32, name="sums")
-        junk = keep.tile([P, PACK * CH], BF16, name="junk")
+        junk = keep.tile([P, PACK * CH], BF16, name="junk", tag="w2_raw", align_bytes=64)
         for c in (0, 1):
             nc.vector.tensor_reduce(sums[:, PACK * c : PACK * (c + 1)], h[c][:], AXIS.X, ALU.add)
         w2_codes = keep.tile([P, N], U32, name="w2_codes", align_bytes=64)

from contextlib import ExitStack

import concourse.mybir as mybir

K, T, S, H, N = 512, 1024, 512, 512, 256
FLOPS = 2 * K * H * S + 2 * H * N * S

F32 = mybir.dt.float32
BF16 = mybir.dt.bfloat16
I32 = mybir.dt.int32
U32 = mybir.dt.uint32
U16 = mybir.dt.uint16
U8 = mybir.dt.uint8
FP8X4 = mybir.dt.float8_e4m3fn_x4
ACT = mybir.ActivationFunctionType
ALU = mybir.AluOpType
AXIS = mybir.AxisListType

P = 128
PACK = 4
CH = 128
NCH = S // CH
LIST_COLS = CH // 16


def tile_picked_deepset_none_p_kernel(tc, x_words, x_scales, w1, w2, offs, out):
    nc = tc.nc
    with ExitStack() as ctx:
        keep = ctx.enter_context(tc.tile_pool(name="keep", bufs=1))
        reuse = ctx.enter_context(tc.tile_pool(name="reuse", bufs=1))
        psum = ctx.enter_context(tc.psum_pool(name="psum", bufs=1))

        offsets = keep.tile([P, S // 16], U16, name="offsets")
        xs_table = reuse.tile([P, T], U8, name="xs_table", offset=0, align_bytes=64)
        xw_table = keep.tile([P, T], I32, name="xw_table", align_bytes=64)
        w1_raw = [keep.tile([P, PACK, H // 2], F32, name="w1_raw%d" % u, align_bytes=64) for u in range(2)]
        w2_raw = keep.tile([P, PACK, N], F32, name="w2_raw", tag="w2_raw", align_bytes=64)

        nc.vector.memset(xs_table[:].bitcast(I32), 0)
        w1_rows = w1.rearrange("(p j) c -> p j c", j=PACK)
        nc.sync.dma_start(w1_raw[0][:], w1_rows[:, :, : H // 2])
        nc.sync.dma_start(offsets[:], offs)
        for q in range(4):
            nc.sync.dma_start(
                xs_table[32 * q : 32 * q + 4, :].bitcast(I32), x_scales[0, 4 * q : 4 * q + 4, :].bitcast(I32)
            )
        nc.sync.dma_start(w1_raw[1][:], w1_rows[:, :, H // 2 :])
        nc.sync.dma_start(xw_table[:], x_words[0].rearrange("p n t -> p (n t)").bitcast(I32))
        w2_rows = w2.rearrange("(g t r) n -> t g r n", t=PACK, r=4)
        for t in range(PACK):
            nc.sync.dma_start(w2_raw[:, t, :], w2_rows[t])

        xs = keep.tile([P, S], U8, name="xs", align_bytes=64)
        nc.vector.tensor_copy(xs[:], xs_table[:].indirect(offsets[:]))

        w1_bf = {}

        def deal_w1(copy, u, t0, t1, dealt):
            copy(
                dealt[:].rearrange("p (t g r j) -> p g t j r", g=16, r=4, j=PACK),
                w1_raw[u][:].rearrange("p j (g t r) -> p g t j r", t=PACK, r=4)[:, :, t0:t1],
            )
            for t in range(t0, t1):
                w1_bf[u, t] = dealt[:, (t - t0) * 256 : (t - t0 + 1) * 256]

        w1_first = keep.tile([P, 1024], BF16, name="w1_first", align_bytes=64)
        w1_middle = reuse.tile([P, 512], BF16, name="w1_middle", offset=512, align_bytes=64)
        w1_last = keep.tile([P, 512], BF16, name="w1_last", tag="w1_last", align_bytes=64)
        deal_w1(nc.scalar.copy, 0, 0, 4, w1_first)
        deal_w1(nc.vector.tensor_copy, 1, 0, 2, w1_middle)
        deal_w1(nc.scalar.copy, 1, 2, 4, w1_last)
        w1_codes = [keep.tile([P, P], U32, name="w1_codes%d" % t, align_bytes=64) for t in range(PACK)]
        w1_scales = reuse.tile([P, H], U8, name="w1_scales", offset=0, align_bytes=64)
        for u, t in ((0, 0), (0, 1), (0, 2), (0, 3), (1, 0), (1, 1), (1, 2), (1, 3)):
            cols = slice(64 * u, 64 * (u + 1))
            nc.vector.quantize_mx(
                out=w1_codes[t][:, cols].bitcast(FP8X4), scales=w1_scales[:, t * P + 64 * u : t * P + 64 * (u + 1)], in_=w1_bf[u, t]
            )

        xw_first = reuse.tile([P, CH], U32, name="xw_first", offset=512, align_bytes=64)
        xw_rest = keep.tile([P, S - CH], U32, name="xw_rest", tag="w1_last", align_bytes=64)
        xw = [xw_first[:]] + [xw_rest[:, c * CH : (c + 1) * CH] for c in range(NCH - 1)]
        for c in range(NCH):
            nc.vector.tensor_copy(
                xw[c],
                xw_table[:].bitcast(U32).indirect(offsets[:, c * LIST_COLS : (c + 1) * LIST_COLS]),
            )

        def first_product(dst, t, c):
            nc.tensor.matmul_mx(
                out=dst,
                lhsT=w1_codes[t][:].bitcast(FP8X4),
                lhsT_scale=w1_scales[:, t * P : (t + 1) * P],
                rhs=xw[c].bitcast(FP8X4),
                rhs_scale=xs[:, c * CH : (c + 1) * CH],
                start=True,
                stop=True,
            )

        last = NCH - 1
        h = []
        for c in range(last):
            bank = psum.tile([P, PACK, CH], F32, name="h%d" % c, tag="bank%d" % c)
            for t in range(PACK):
                first_product(bank[:, t, :], t, c)
            h.append(bank)
        h_last = []
        for u in range(2):
            bank = psum.tile([P, 2, CH], F32, name="h_last%d" % u, tag="bank%d" % (last + u))
            for e in range(2):
                first_product(bank[:, e, :], 2 * u + e, last)
            h_last.append(bank)

        w2_bf = keep.tile([P, N * PACK], BF16, name="w2_bf", align_bytes=64)
        nc.scalar.copy(
            w2_bf[:].rearrange("p (a i j) -> p a j i", i=4, j=PACK),
            w2_raw[:].rearrange("p j (a i) -> p a j i", i=4),
        )

        sums = keep.tile([P, NCH * PACK], F32, name="sums")
        junk = keep.tile([P, PACK * CH], BF16, name="junk", tag="w2_raw", align_bytes=64)
        for c in (0, 1):
            nc.vector.tensor_reduce(sums[:, PACK * c : PACK * (c + 1)], h[c][:], AXIS.X, ALU.add)
        w2_codes = keep.tile([P, N], U32, name="w2_codes", align_bytes=64)
        w2_scales = keep.tile([P, N], U8, name="w2_scales", align_bytes=64)
        nc.vector.quantize_mx(out=w2_codes[:].bitcast(FP8X4), scales=w2_scales[:], in_=w2_bf[:])
        for t in range(PACK):
            nc.scalar.activation(
                junk[:, t * CH : (t + 1) * CH], h[2][:, t, :], ACT.Copy, accum_out=sums[:, 8 + t : 9 + t]
            )
        for u in range(2):
            nc.vector.tensor_reduce(sums[:, 12 + 2 * u : 14 + 2 * u], h_last[u][:], AXIS.X, ALU.add)

        total = keep.tile([P, PACK], F32, name="total")
        nc.vector.tensor_reduce(total[:], sums[:].rearrange("p (c t) -> p t c", t=PACK), AXIS.X, ALU.add)

        neg_mean = keep.tile([P, PACK], F32, name="neg_mean")
        nc.scalar.activation(neg_mean[:], total[:], ACT.Copy, scale=-1.0 / S)

        z_bf = [keep.tile([P, CH * PACK], BF16, name="z_bf%d" % c, align_bytes=64) for c in range(NCH)]
        out_rows = out.rearrange("(a p) s -> p a s", p=P)

        def centre_on_vector(c):
            nc.vector.scalar_tensor_tensor(
                out=z_bf[c][:].rearrange("p (n t) -> p n t", t=PACK),
                in0=total[:].unsqueeze(1).to_broadcast([P, CH, PACK]),
                scalar=-1.0 / S,
                in1=h[c][:].rearrange("p t n -> p n t"),
                op0=ALU.mult,
                op1=ALU.add,
            )

        planes = keep.tile([P, PACK * CH], BF16, name="planes", align_bytes=64)
        for t in range(PACK):
            nc.scalar.activation(
                planes[:, t * CH : (t + 1) * CH], h_last[t // 2][:, t % 2, :], ACT.Identity, bias=neg_mean[:, t : t + 1]
            )
        nc.scalar.copy(
            z_bf[last][:].rearrange("p (a i t) -> p a t i", i=4, t=PACK),
            planes[:].rearrange("p (t a i) -> p a t i", t=PACK, i=4),
        )

        def second_product(c, dsts):
            z_codes = keep.tile([P, CH], U32, name="z_codes%d" % c, align_bytes=64)
            z_scales = keep.tile([P, CH], U8, name="z_scales%d" % c, align_bytes=64)
            nc.vector.quantize_mx(out=z_codes[:].bitcast(FP8X4), scales=z_scales[:], in_=z_bf[c][:])
            for a in range(N // P):
                nc.tensor.matmul_mx(
                    out=dsts[a],
                    lhsT=w2_codes[:, a * P : (a + 1) * P].bitcast(FP8X4),
                    lhsT_scale=w2_scales[:, a * P : (a + 1) * P],
                    rhs=z_codes[:].bitcast(FP8X4),
                    rhs_scale=z_scales[:],
                    start=True,
                    stop=True,
                )

        def finish(c):
            bank = psum.tile([P, N // P, CH], F32, name="o%d" % c, tag="obank%d" % c)
            second_product(c, [bank[:, 0, :], bank[:, 1, :]])
            result = keep.tile([P, N // P, CH], F32, name="result%d" % c)
            nc.scalar.copy(result[:], bank[:])
            nc.sync.dma_start(out_rows[:, :, c * CH : (c + 1) * CH], result[:])

        def finish_split(c):
            halves = [psum.tile([P, CH], F32, name="o%d_%d" % (c, a), tag="bank%d" % a) for a in range(2)]
            second_product(c, [halves[0][:], halves[1][:]])
            results = [keep.tile([P, CH], F32, name="result%d_%d" % (c, a)) for a in range(2)]
            nc.vector.tensor_copy(results[0][:], halves[0][:])
            nc.sync.dma_start(out_rows[:, 0, c * CH : (c + 1) * CH], results[0][:])
            nc.scalar.copy(results[1][:], halves[1][:])
            nc.scalar.dma_start(out_rows[:, 1, c * CH : (c + 1) * CH], results[1][:])

        centre_on_vector(0)
        centre_on_vector(1)
        finish(0)
        finish(1)
        centre_on_vector(2)
        finish(3)
        finish_split(2)
